import numpy as np
import ml_dtypes


def mxq(x, axis, fmt="e4m3"):
    dtype, down = {"e4m3": (ml_dtypes.float8_e4m3fn, 7), "e5m2": (ml_dtypes.float8_e5m2, 14)}[fmt]
    v = np.moveaxis(np.asarray(x, np.float32).astype(ml_dtypes.bfloat16).astype(np.float64), axis, -1)
    blocks = v.reshape(v.shape[:-1] + (-1, 32))
    amax = np.abs(blocks).max(-1, keepdims=True)
    byte = np.maximum(np.where(amax > 0, np.frexp(amax)[1] - 1 + 127, 0) - down, 1)
    scale = np.exp2(byte - 127.0)
    codes = (blocks / scale).astype(np.float32).astype(dtype).astype(np.float64)
    return np.moveaxis((codes * scale).reshape(v.shape), -1, axis)


WIDE = False


def mx_kscale(k):
    if not WIDE:
        return np.ones(k)
    levels = np.array([10, -10, 5, -5, 0])
    if k % 512:
        return np.exp2(np.random.permutation(np.resize(levels, k // 32))).repeat(32)
    a = np.empty((k // 512, 16))
    for p in range(k // 512):
        a[p, :8] = np.random.permutation(np.resize(levels, 8))
        for g in range(8):
            far = levels[np.abs(levels - a[p, g]) >= 10]
            a[p, g + 8] = far[np.random.randint(len(far))]
    return np.exp2(a.ravel()).repeat(32)


def f64(x):
    return np.asarray(x).astype(np.float64)


def striped(idx):
    return np.tile(idx.reshape(-1, 16).T, (8, 1)).astype(np.uint16)


def unstriped(offs):
    return offs[:16].T.reshape(-1).astype(np.int64)


def relu2(v):
    return np.maximum(v, 0.0) ** 2


K, T, E, C, N = 1024, 1280, 4, 256, 256


def by_expert(wq, xq):
    return np.concatenate([wq[e].T @ xq[:, e * C:(e + 1) * C] for e in range(E)], axis=1)


def setup_inputs():
    n = np.random.standard_normal
    s = mx_kscale(K)[:, None]
    return {
        "xT": (n((K, T)) * s).astype(np.float32),
        "xr": n((N, T)).astype(np.float32),
        "w": (n((E, K, N)) / np.sqrt(K) / s[None]).astype(np.float32),
        "b": (0.3 * n((N, E))).astype(np.float32),
        "gate": np.tile(np.random.uniform(0.2, 1.0, E * C), (N, 1)).astype(np.float32),
        "offs": striped(np.random.permutation(T)[:E * C]),
    }


def reference(xT, xr, w, b, gate, offs):
    idx = unstriped(offs)
    xq = mxq(f64(xT)[:, idx], 0, "e4m3")
    y = by_expert(mxq(f64(w), 1, "e4m3"), xq)
    y = relu2(y + np.repeat(f64(b), C, axis=1))
    out = f64(xr).copy()
    out[:, idx] += f64(gate) * y
    return out

@@ -1,0 +1,214 @@
+from contextlib import ExitStack
+
+import concourse.mybir as mybir
+
+K, T, E, C, N = 1024, 1280, 4, 256, 256
+P = 128
+PACK = 4
+PASSES = K // (P * PACK)
+HALVES = N // P
+FLOPS = 2 * K * N * E * C
+
+F32 = mybir.dt.float32
+BF16 = mybir.dt.bfloat16
+U32 = mybir.dt.uint32
+U16 = mybir.dt.uint16
+U8 = mybir.dt.uint8
+FP8X4 = mybir.dt.float8_e4m3fn_x4
+ADD, MULT = mybir.AluOpType.add, mybir.AluOpType.mult
+COPY = mybir.ActivationFunctionType.Copy
+RELU = mybir.ActivationFunctionType.Relu
+SQUARE = mybir.ActivationFunctionType.Square
+
+X_CHUNKS = [
+    (0, 0, [("v", 256)]),
+    (0, 256, [("s", 256), ("v", 256)]),
+    (0, 768, [("s", 128), ("v", 256), ("v", 128)]),
+    (1, 0, [("s", 256), ("v", 256)]),
+    (1, 512, [("s", 256), ("v", 256)]),
+    (1, 1024, [("s", 128), ("v", 128)]),
+]
+
+
+def interleaved(view):
+    return view.rearrange("p (c i) t -> p c t i", i=4)
+
+
+def rows(view):
+    return view.rearrange("p t (c i) -> p c t i", i=4)
+
+
+def tile_moe_res_lin_relu2_kernel(tc, xT, xr, w, b, gate, offs, out):
+    nc = tc.nc
+    x_view = xT.rearrange("(a p j) t -> a p j t", p=P, j=PACK)
+    w_view = w.rearrange("e (a p j) n -> e a p j n", p=P, j=PACK)
+    xr_view = xr.rearrange("(h p) t -> h p t", p=P)
+    gate_view = gate.rearrange("(h p) s -> h p s", p=P)
+    out_view = out.rearrange("(h p) t -> h p t", p=P)
+
+    with ExitStack() as ctx:
+        keep = ctx.enter_context(tc.tile_pool(name="keep", bufs=1))
+        psum = ctx.enter_context(tc.psum_pool(name="psum", bufs=1))
+
+        offs_sb = keep.tile([P, E * C // 16], U16, name="offs_sb")
+        x_codes = [keep.tile([P, T], U32, name=f"x_codes{a}", align_bytes=64) for a in range(PASSES)]
+        x_scales = keep.tile([P, T], U8, name="x_scales", align_bytes=64)
+        window = [keep.tile([P, T], F32, name=f"window{h}") for h in range(HALVES)]
+
+        nc.gpsimd.memset(x_scales[:], 0)
+        for h in range(HALVES):
+            nc.gpsimd.memset(window[h][:], 0.0)
+
+        x_raw = []
+        for i, (a, t0, pieces) in enumerate(X_CHUNKS):
+            n = sum(m for eng, m in pieces)
+            raw = keep.tile([P, PACK, n], F32, name=f"x_raw{i}")
+            nc.sync.dma_start(out=raw[:], in_=x_view[a][:, :, t0 : t0 + n])
+            x_raw.append(raw)
+            if i == 1:
+                nc.sync.dma_start(offs_sb[:], offs)
+        w_raw = {}
+        gate_sb = {}
+        xr_sb = [keep.tile([P, T], F32, name=f"xr{h}") for h in range(HALVES)]
+        b_sb = keep.tile([P, HALVES, E], F32, name="b_sb")
+
+        def load_w(e, a):
+            raw = keep.tile([P, PACK, N], F32, name=f"w_raw{e}_{a}")
+            nc.sync.dma_start(out=raw[:], in_=w_view[e, a])
+            w_raw[e, a] = raw
+
+        def load_gate(h, e0, e1):
+            g = keep.tile([P, (e1 - e0) * C], F32, name=f"gate{h}_{e0}")
+            nc.sync.dma_start(out=g[:], in_=gate_view[h][:, e0 * C : e1 * C])
+            for e in range(e0, e1):
+                gate_sb[e, h] = g[:, (e - e0) * C : (e - e0 + 1) * C]
+
+        load_w(0, 0)
+        load_w(0, 1)
+        nc.sync.dma_start(out=b_sb[:], in_=b.rearrange("(h p) e -> p h e", p=P))
+        load_w(1, 0)
+        load_w(1, 1)
+        load_w(2, 0)
+        load_gate(0, 0, 2)
+        load_gate(1, 0, 1)
+        load_w(2, 1)
+        load_w(3, 0)
+        load_w(3, 1)
+        load_gate(0, 2, 4)
+        load_gate(1, 1, 4)
+        for h in range(HALVES):
+            nc.sync.dma_start(out=xr_sb[h][:], in_=xr_view[h])
+
+        x_words = {}
+
+        def gather_words(a, s0, n, tag=None):
+            got = keep.tile([P, n], U32, name=f"words{a}_{s0}", tag=tag or f"words{a}_{s0}", align_bytes=64)
+            nc.vector.tensor_copy(got[:], x_codes[a][:].indirect(offs_sb[:, s0 // 16 : (s0 + n) // 16]))
+            for e in range(s0 // C, (s0 + n) // C):
+                x_words[a, e] = got[:, e * C - s0 : (e + 1) * C - s0]
+
+        x_bytes = {}
+
+        def gather_bytes(s0, n):
+            got = keep.tile([P, n], U8, name=f"bytes_{s0}", align_bytes=64)
+            nc.vector.tensor_copy(got[:], x_scales[:].indirect(offs_sb[:, s0 // 16 : (s0 + n) // 16]))
+            for e in range(s0 // C, (s0 + n) // C):
+                for a in range(PASSES):
+                    x_bytes[a, e] = got[4 * a :, e * C - s0 : (e + 1) * C - s0]
+
+        for i, (a, t0, pieces) in enumerate(X_CHUNKS):
+            units = []
+            u0 = 0
+            for eng, m in pieces:
+                bf = keep.tile([P, m, PACK], BF16, name=f"x_bf{i}_{u0}", align_bytes=64)
+                dst = interleaved(bf[:])
+                src = rows(x_raw[i][:, :, u0 : u0 + m])
+                if eng == "s":
+                    nc.scalar.activation(dst, src, COPY)
+                else:
+                    nc.vector.tensor_copy(dst, src)
+                units.append((u0, m, bf))
+                u0 += m
+            for u0, m, bf in units[1:] + units[:1]:
+                cols = slice(t0 + u0, t0 + u0 + m)
+                nc.vector.quantize_mx(
+                    out=x_codes[a][:, cols].bitcast(FP8X4),
+                    scales=x_scales[4 * a :, cols],
+                    in_=bf[:].rearrange("p n t -> p (n t)"),
+                )
+            if i == 2:
+                gather_words(0, 0, 512)
+                gather_words(0, 512, 512)
+
+        w_codes, w_scales = [], []
+
+        def weights(e):
+            bf = keep.tile([P, PASSES, N, PACK], BF16, name=f"w_bf{e}", tag=f"w_bf{e}", align_bytes=64)
+            for a in range(PASSES):
+                if (e, a) == (1, 1):
+                    nc.gpsimd.tensor_scalar(interleaved(bf[:, a]), rows(w_raw[e, a][:]), 1.0, 0.0, MULT, ADD)
+                else:
+                    nc.scalar.activation(interleaved(bf[:, a]), rows(w_raw[e, a][:]), COPY)
+            codes = keep.tile([P, PASSES * N], U32, name=f"w_codes{e}", align_bytes=64)
+            scales = keep.tile([P, PASSES * N], U8, name=f"w_scales{e}", align_bytes=64)
+            nc.vector.quantize_mx(
+                out=codes[:].bitcast(FP8X4), scales=scales[:], in_=bf[:].rearrange("p a n t -> p (a n t)")
+            )
+            w_codes.append(codes)
+            w_scales.append(scales)
+
+        squares = []
+
+        def expert(e):
+            accs = []
+            for h in range(HALVES):
+                acc = psum.tile([P, C], F32, name=f"acc{e}_{h}")
+                accs.append(acc)
+                for a in range(PASSES):
+                    cols = slice(a * N + h * P, a * N + (h + 1) * P)
+                    nc.tensor.matmul_mx(
+                        out=acc[:],
+                        lhsT=w_codes[e][:, cols].bitcast(FP8X4),
+                        lhsT_scale=w_scales[e][:, cols],
+                        rhs=x_words[a, e].bitcast(FP8X4),
+                        rhs_scale=x_bytes[a, e],
+                        start=(a == 0),
+                        stop=(a == PASSES - 1),
+                    )
+            r = keep.tile([P, HALVES * C], F32, name=f"relu{e}")
+            s = keep.tile([P, HALVES * C], F32, name=f"square{e}")
+            for h in range(HALVES):
+                cols = slice(h * C, (h + 1) * C)
+                nc.scalar.activation(r[:, cols], accs[h][:], RELU, bias=b_sb[:, h, e : e + 1])
+                nc.scalar.activation(s[:, cols], r[:, cols], SQUARE)
+            squares.append(s)
+
+        def scatter(e, h):
+            nc.vector.tensor_tensor(
+                window[h][:].indirect(offs_sb[:, e * C // 16 : (e + 1) * C // 16]),
+                squares[e][:, h * C : (h + 1) * C],
+                gate_sb[e, h],
+                MULT,
+            )
+
+        for e in range(2):
+            gather_words(1, e * C, C)
+            gather_bytes(e * C, C)
+        weights(0)
+        expert(0)
+        weights(1)
+        gather_words(1, 512, 512, tag="w_bf0")
+        gather_bytes(512, 512)
+        expert(1)
+        for e in range(E):
+            scatter(e, 0)
+            if 1 <= e < E - 1:
+                weights(e + 1)
+                expert(e + 1)
+            scatter(e, 1)
+        for h in range(HALVES):
+            o = keep.tile([P, T], F32, name=f"o{h}")
+            for t0 in range(0, T, T // 2):
+                cols = slice(t0, t0 + T // 2)
+                nc.vector.tensor_tensor(o[:, cols], window[h][:, cols], xr_sb[h][:, cols], ADD)
+                nc.sync.dma_start(out=out_view[h][:, cols], in_=o[:, cols])

@@ -157,7 +157,7 @@ def tile_moe_res_lin_relu2_kernel(tc, xT, xr, w, b, gate, offs, out):
             w_codes.append(codes)
             w_scales.append(scales)
 
-        squares = []
+        gated = {}
 
         def expert(e):
             accs = []
@@ -181,15 +181,12 @@ def tile_moe_res_lin_relu2_kernel(tc, xT, xr, w, b, gate, offs, out):
                 cols = slice(h * C, (h + 1) * C)
                 nc.scalar.activation(r[:, cols], accs[h][:], RELU, bias=b_sb[:, h, e : e + 1])
                 nc.scalar.activation(s[:, cols], r[:, cols], SQUARE)
-            squares.append(s)
+                g = keep.tile([P, C], F32, name=f"gated{e}_{h}")
+                nc.gpsimd.tensor_tensor(g[:], s[:, cols], gate_sb[e, h], MULT)
+                gated[e, h] = g
 
         def scatter(e, h):
-            nc.vector.tensor_tensor(
-                window[h][:].indirect(offs_sb[:, e * C // 16 : (e + 1) * C // 16]),
-                squares[e][:, h * C : (h + 1) * C],
-                gate_sb[e, h],
-                MULT,
-            )
+            nc.vector.tensor_copy(window[h][:].indirect(offs_sb[:, e * C // 16 : (e + 1) * C // 16]), gated[e, h][:])
 
         for e in range(2):
             gather_words(1, e * C, C)
@@ -200,15 +197,24 @@ def tile_moe_res_lin_relu2_kernel(tc, xT, xr, w, b, gate, offs, out):
         gather_words(1, 512, 512, tag="w_bf0")
         gather_bytes(512, 512)
         expert(1)
-        for e in range(E):
-            scatter(e, 0)
-            if 1 <= e < E - 1:
-                weights(e + 1)
-                expert(e + 1)
-            scatter(e, 1)
-        for h in range(HALVES):
+        def finish(engine, h, pieces):
             o = keep.tile([P, T], F32, name=f"o{h}")
-            for t0 in range(0, T, T // 2):
-                cols = slice(t0, t0 + T // 2)
-                nc.vector.tensor_tensor(o[:, cols], window[h][:, cols], xr_sb[h][:, cols], ADD)
+            for t0 in range(0, T, T // pieces):
+                cols = slice(t0, t0 + T // pieces)
+                engine.tensor_tensor(o[:, cols], window[h][:, cols], xr_sb[h][:, cols], ADD)
                 nc.sync.dma_start(out=out_view[h][:, cols], in_=o[:, cols])
+
+        scatter(0, 0)
+        scatter(0, 1)
+        weights(2)
+        expert(2)
+        scatter(1, 0)
+        scatter(1, 1)
+        weights(3)
+        expert(3)
+        scatter(2, 0)
+        scatter(3, 0)
+        finish(nc.gpsimd, 0, 2)
+        scatter(2, 1)
+        scatter(3, 1)
+        finish(nc.vector, 1, 2)

@@ -21,13 +21,15 @@ RELU = mybir.ActivationFunctionType.Relu
 SQUARE = mybir.ActivationFunctionType.Square
 
 X_CHUNKS = [
-    (0, 0, [("v", 256)]),
-    (0, 256, [("s", 256), ("v", 256)]),
-    (0, 768, [("s", 128), ("v", 256), ("v", 128)]),
-    (1, 0, [("s", 256), ("v", 256)]),
+    (0, 0, [("s", 256), ("v", 256)]),
+    (0, 512, [("s", 256), ("v", 256)]),
+    (0, 1024, [("v", 256)]),
+    (1, 0, [("s", 384), ("v", 128)]),
     (1, 512, [("s", 256), ("v", 256)]),
     (1, 1024, [("s", 128), ("v", 128)]),
 ]
+
+AFTER = {(0, 0): "w_raw1_0", (0, 1): "w_raw1_1", (1, 0): "w_raw2_1", (2, 0): "w_raw3_1"}
 
 
 def interleaved(view):
@@ -54,26 +56,24 @@ def tile_moe_res_lin_relu2_kernel(tc, xT, xr, w, b, gate, offs, out):
         x_codes = [keep.tile([P, T], U32, name=f"x_codes{a}", align_bytes=64) for a in range(PASSES)]
         x_scales = keep.tile([P, T], U8, name="x_scales", align_bytes=64)
         window = [keep.tile([P, T], F32, name=f"window{h}") for h in range(HALVES)]
+        xr_sb = [keep.tile([P, T], F32, name=f"xr{h}") for h in range(HALVES)]
+        b_sb = keep.tile([P, HALVES, E], F32, name="b_sb")
 
         nc.gpsimd.memset(x_scales[:], 0)
         for h in range(HALVES):
             nc.gpsimd.memset(window[h][:], 0.0)
 
-        x_raw = []
-        for i, (a, t0, pieces) in enumerate(X_CHUNKS):
+        x_raw, w_raw, gate_sb = [], {}, {}
+
+        def load_x(i):
+            a, t0, pieces = X_CHUNKS[i]
             n = sum(m for eng, m in pieces)
             raw = keep.tile([P, PACK, n], F32, name=f"x_raw{i}")
             nc.sync.dma_start(out=raw[:], in_=x_view[a][:, :, t0 : t0 + n])
             x_raw.append(raw)
-            if i == 1:
-                nc.sync.dma_start(offs_sb[:], offs)
-        w_raw = {}
-        gate_sb = {}
-        xr_sb = [keep.tile([P, T], F32, name=f"xr{h}") for h in range(HALVES)]
-        b_sb = keep.tile([P, HALVES, E], F32, name="b_sb")
 
         def load_w(e, a):
-            raw = keep.tile([P, PACK, N], F32, name=f"w_raw{e}_{a}")
+            raw = keep.tile([P, PACK, N], F32, name=f"w_raw{e}_{a}", tag=f"w_raw{e}_{a}")
             nc.sync.dma_start(out=raw[:], in_=w_view[e, a])
             w_raw[e, a] = raw
 
@@ -83,23 +83,36 @@ def tile_moe_res_lin_relu2_kernel(tc, xT, xr, w, b, gate, offs, out):
             for e in range(e0, e1):
                 gate_sb[e, h] = g[:, (e - e0) * C : (e - e0 + 1) * C]
 
+        def load_xr(h):
+            nc.sync.dma_start(out=xr_sb[h][:], in_=xr_view[h])
+
+        def load_b():
+            nc.sync.dma_start(out=b_sb[:], in_=b.rearrange("(h p) e -> p h e", p=P))
+
+        load_x(0)
+        load_x(1)
+        nc.sync.dma_start(offs_sb[:], offs)
+        load_x(2)
+        load_x(3)
+        load_x(4)
+        load_x(5)
         load_w(0, 0)
         load_w(0, 1)
-        nc.sync.dma_start(out=b_sb[:], in_=b.rearrange("(h p) e -> p h e", p=P))
+        load_b()
         load_w(1, 0)
         load_w(1, 1)
-        load_w(2, 0)
         load_gate(0, 0, 2)
-        load_gate(1, 0, 1)
+        load_gate(1, 0, 2)
+        load_w(2, 0)
         load_w(2, 1)
         load_w(3, 0)
         load_w(3, 1)
         load_gate(0, 2, 4)
-        load_gate(1, 1, 4)
-        for h in range(HALVES):
-            nc.sync.dma_start(out=xr_sb[h][:], in_=xr_view[h])
+        load_gate(1, 2, 4)
+        load_xr(0)
+        load_xr(1)
 
-        x_words = {}
+        x_words, x_bytes = {}, {}
 
         def gather_words(a, s0, n, tag=None):
             got = keep.tile([P, n], U32, name=f"words{a}_{s0}", tag=tag or f"words{a}_{s0}", align_bytes=64)
@@ -107,57 +120,61 @@ def tile_moe_res_lin_relu2_kernel(tc, xT, xr, w, b, gate, offs, out):
             for e in range(s0 // C, (s0 + n) // C):
                 x_words[a, e] = got[:, e * C - s0 : (e + 1) * C - s0]
 
-        x_bytes = {}
-
-        def gather_bytes(s0, n):
-            got = keep.tile([P, n], U8, name=f"bytes_{s0}", align_bytes=64)
+        def gather_bytes(s0, n, tag=None):
+            got = keep.tile([P, n], U8, name=f"bytes_{s0}", tag=tag or f"bytes_{s0}", align_bytes=64)
             nc.vector.tensor_copy(got[:], x_scales[:].indirect(offs_sb[:, s0 // 16 : (s0 + n) // 16]))
             for e in range(s0 // C, (s0 + n) // C):
                 for a in range(PASSES):
                     x_bytes[a, e] = got[4 * a :, e * C - s0 : (e + 1) * C - s0]
 
-        for i, (a, t0, pieces) in enumerate(X_CHUNKS):
-            units = []
+        x_bf = {}
+
+        def lay_x(i):
+            a, t0, pieces = X_CHUNKS[i]
+            n = sum(m for eng, m in pieces)
+            bf = keep.tile([P, n, PACK], BF16, name=f"x_bf{i}", align_bytes=64)
             u0 = 0
             for eng, m in pieces:
-                bf = keep.tile([P, m, PACK], BF16, name=f"x_bf{i}_{u0}", align_bytes=64)
-                dst = interleaved(bf[:])
+                dst = interleaved(bf[:, u0 : u0 + m, :])
                 src = rows(x_raw[i][:, :, u0 : u0 + m])
                 if eng == "s":
                     nc.scalar.activation(dst, src, COPY)
                 else:
                     nc.vector.tensor_copy(dst, src)
-                units.append((u0, m, bf))
                 u0 += m
-            for u0, m, bf in units[1:] + units[:1]:
-                cols = slice(t0 + u0, t0 + u0 + m)
-                nc.vector.quantize_mx(
-                    out=x_codes[a][:, cols].bitcast(FP8X4),
-                    scales=x_scales[4 * a :, cols],
-                    in_=bf[:].rearrange("p n t -> p (n t)"),
-                )
-            if i == 2:
-                gather_words(0, 0, 512)
-                gather_words(0, 512, 512)
+            x_bf[i] = bf
 
-        w_codes, w_scales = [], []
+        def quantise_x(i):
+            a, t0, pieces = X_CHUNKS[i]
+            n = sum(m for eng, m in pieces)
+            cols = slice(t0, t0 + n)
+            nc.vector.quantize_mx(
+                out=x_codes[a][:, cols].bitcast(FP8X4),
+                scales=x_scales[4 * a :, cols],
+                in_=x_bf[i][:].rearrange("p n t -> p (n t)"),
+            )
+
+        w_codes, w_scales = {}, {}
 
         def weights(e):
             bf = keep.tile([P, PASSES, N, PACK], BF16, name=f"w_bf{e}", tag=f"w_bf{e}", align_bytes=64)
             for a in range(PASSES):
-                if (e, a) == (1, 1):
+                if (e, a) in ():
                     nc.gpsimd.tensor_scalar(interleaved(bf[:, a]), rows(w_raw[e, a][:]), 1.0, 0.0, MULT, ADD)
+                elif (e, a) in ():
+                    nc.vector.tensor_copy(interleaved(bf[:, a]), rows(w_raw[e, a][:]))
                 else:
-                    nc.scalar.activation(interleaved(bf[:, a]), rows(w_raw[e, a][:]), COPY)
+                    for n0 in range(0, N, 256):
+                        cols = slice(n0, n0 + 256)
+                        nc.scalar.activation(interleaved(bf[:, a, cols, :]), rows(w_raw[e, a][:, :, cols]), COPY)
             codes = keep.tile([P, PASSES * N], U32, name=f"w_codes{e}", align_bytes=64)
             scales = keep.tile([P, PASSES * N], U8, name=f"w_scales{e}", align_bytes=64)
             nc.vector.quantize_mx(
                 out=codes[:].bitcast(FP8X4), scales=scales[:], in_=bf[:].rearrange("p a n t -> p (a n t)")
             )
-            w_codes.append(codes)
-            w_scales.append(scales)
+            w_codes[e], w_scales[e] = codes, scales
 
-        gated = {}
+        squares = {}
 
         def expert(e):
             accs = []
@@ -175,46 +192,57 @@ def tile_moe_res_lin_relu2_kernel(tc, xT, xr, w, b, gate, offs, out):
                         start=(a == 0),
                         stop=(a == PASSES - 1),
                     )
-            r = keep.tile([P, HALVES * C], F32, name=f"relu{e}")
-            s = keep.tile([P, HALVES * C], F32, name=f"square{e}")
             for h in range(HALVES):
-                cols = slice(h * C, (h + 1) * C)
-                nc.scalar.activation(r[:, cols], accs[h][:], RELU, bias=b_sb[:, h, e : e + 1])
-                nc.scalar.activation(s[:, cols], r[:, cols], SQUARE)
-                g = keep.tile([P, C], F32, name=f"gated{e}_{h}")
-                nc.gpsimd.tensor_tensor(g[:], s[:, cols], gate_sb[e, h], MULT)
-                gated[e, h] = g
+                r = keep.tile([P, C], F32, name=f"relu{e}_{h}", tag=AFTER.get((e, h), f"relu{e}_{h}"))
+                s = keep.tile([P, C], F32, name=f"square{e}_{h}")
+                nc.scalar.activation(r[:], accs[h][:], RELU, bias=b_sb[:, h, e : e + 1])
+                nc.scalar.activation(s[:], r[:], SQUARE)
+                squares[e, h] = s
 
         def scatter(e, h):
-            nc.vector.tensor_copy(window[h][:].indirect(offs_sb[:, e * C // 16 : (e + 1) * C // 16]), gated[e, h][:])
+            nc.vector.tensor_tensor(
+                window[h][:].indirect(offs_sb[:, e * C // 16 : (e + 1) * C // 16]), squares[e, h][:], gate_sb[e, h], MULT
+            )
 
-        for e in range(2):
-            gather_words(1, e * C, C)
-            gather_bytes(e * C, C)
-        weights(0)
-        expert(0)
-        weights(1)
-        gather_words(1, 512, 512, tag="w_bf0")
-        gather_bytes(512, 512)
-        expert(1)
-        def finish(engine, h, pieces):
+        def finish(h, widths):
             o = keep.tile([P, T], F32, name=f"o{h}")
-            for t0 in range(0, T, T // pieces):
-                cols = slice(t0, t0 + T // pieces)
-                engine.tensor_tensor(o[:, cols], window[h][:, cols], xr_sb[h][:, cols], ADD)
+            t0 = 0
+            for n in widths:
+                cols = slice(t0, t0 + n)
+                nc.vector.tensor_tensor(o[:, cols], window[h][:, cols], xr_sb[h][:, cols], ADD)
                 nc.sync.dma_start(out=out_view[h][:, cols], in_=o[:, cols])
+                t0 += n
 
+        for i in range(3):
+            lay_x(i)
+            quantise_x(i)
+        gather_words(0, 0, 512)
+        gather_words(0, 512, 512)
+        lay_x(3)
+        lay_x(4)
+        quantise_x(3)
+        lay_x(5)
+        quantise_x(4)
+        quantise_x(5)
+        gather_words(1, 0, 256)
+        gather_bytes(0, 256)
+        gather_words(1, 256, 768)
+        weights(0)
+        gather_bytes(256, 768, tag="w_bf0")
+        weights(1)
+        expert(0)
         scatter(0, 0)
-        scatter(0, 1)
         weights(2)
-        expert(2)
+        expert(1)
+        scatter(0, 1)
         scatter(1, 0)
-        scatter(1, 1)
         weights(3)
+        scatter(1, 1)
+        expert(2)
         expert(3)
         scatter(2, 0)
-        scatter(3, 0)
-        finish(nc.gpsimd, 0, 2)
         scatter(2, 1)
+        scatter(3, 0)
         scatter(3, 1)
-        finish(nc.vector, 1, 2)
+        finish(0, (640, 640))
+        finish(1, (512, 512, 256))

@@ -21,9 +21,8 @@ RELU = mybir.ActivationFunctionType.Relu
 SQUARE = mybir.ActivationFunctionType.Square
 
 X_CHUNKS = [
-    (0, 0, [("s", 256), ("v", 256)]),
-    (0, 512, [("s", 256), ("v", 256)]),
-    (0, 1024, [("v", 256)]),
+    (0, 0, [("s", 256), ("v", 512)]),
+    (0, 768, [("v", 256), ("s", 256)]),
     (1, 0, [("s", 384), ("v", 128)]),
     (1, 512, [("s", 256), ("v", 256)]),
     (1, 1024, [("s", 128), ("v", 128)]),
@@ -95,7 +94,6 @@ def tile_moe_res_lin_relu2_kernel(tc, xT, xr, w, b, gate, offs, out):
         load_x(2)
         load_x(3)
         load_x(4)
-        load_x(5)
         load_w(0, 0)
         load_w(0, 1)
         load_b()
@@ -144,14 +142,14 @@ def tile_moe_res_lin_relu2_kernel(tc, xT, xr, w, b, gate, offs, out):
                 u0 += m
             x_bf[i] = bf
 
-        def quantise_x(i):
+        def quantise_x(i, u0=0, n=None):
             a, t0, pieces = X_CHUNKS[i]
-            n = sum(m for eng, m in pieces)
-            cols = slice(t0, t0 + n)
+            n = n or sum(m for eng, m in pieces)
+            cols = slice(t0 + u0, t0 + u0 + n)
             nc.vector.quantize_mx(
                 out=x_codes[a][:, cols].bitcast(FP8X4),
                 scales=x_scales[4 * a :, cols],
-                in_=x_bf[i][:].rearrange("p n t -> p (n t)"),
+                in_=x_bf[i][:, u0 : u0 + n, :].rearrange("p n t -> p (n t)"),
             )
 
         w_codes, w_scales = {}, {}
@@ -174,13 +172,12 @@ def tile_moe_res_lin_relu2_kernel(tc, xT, xr, w, b, gate, offs, out):
             )
             w_codes[e], w_scales[e] = codes, scales
 
-        squares = {}
+        squares, accs = {}, {}
 
-        def expert(e):
-            accs = []
+        def multiply(e):
             for h in range(HALVES):
                 acc = psum.tile([P, C], F32, name=f"acc{e}_{h}")
-                accs.append(acc)
+                accs[e, h] = acc
                 for a in range(PASSES):
                     cols = slice(a * N + h * P, a * N + (h + 1) * P)
                     nc.tensor.matmul_mx(
@@ -192,10 +189,12 @@ def tile_moe_res_lin_relu2_kernel(tc, xT, xr, w, b, gate, offs, out):
                         start=(a == 0),
                         stop=(a == PASSES - 1),
                     )
-            for h in range(HALVES):
+
+        def activate(e, halves=(0, 1)):
+            for h in halves:
                 r = keep.tile([P, C], F32, name=f"relu{e}_{h}", tag=AFTER.get((e, h), f"relu{e}_{h}"))
                 s = keep.tile([P, C], F32, name=f"square{e}_{h}")
-                nc.scalar.activation(r[:], accs[h][:], RELU, bias=b_sb[:, h, e : e + 1])
+                nc.scalar.activation(r[:], accs[e, h][:], RELU, bias=b_sb[:, h, e : e + 1])
                 nc.scalar.activation(s[:], r[:], SQUARE)
                 squares[e, h] = s
 
@@ -204,45 +203,52 @@ def tile_moe_res_lin_relu2_kernel(tc, xT, xr, w, b, gate, offs, out):
                 window[h][:].indirect(offs_sb[:, e * C // 16 : (e + 1) * C // 16]), squares[e, h][:], gate_sb[e, h], MULT
             )
 
-        def finish(h, widths):
-            o = keep.tile([P, T], F32, name=f"o{h}")
-            t0 = 0
+        total = [keep.tile([P, T], F32, name=f"total{h}") for h in range(HALVES)]
+
+        def finish(h, t0, *widths):
             for n in widths:
                 cols = slice(t0, t0 + n)
-                nc.vector.tensor_tensor(o[:, cols], window[h][:, cols], xr_sb[h][:, cols], ADD)
-                nc.sync.dma_start(out=out_view[h][:, cols], in_=o[:, cols])
+                nc.vector.tensor_tensor(total[h][:, cols], window[h][:, cols], xr_sb[h][:, cols], ADD)
+                nc.sync.dma_start(out=out_view[h][:, cols], in_=total[h][:, cols])
                 t0 += n
 
-        for i in range(3):
-            lay_x(i)
-            quantise_x(i)
+        lay_x(0)
+        quantise_x(0, 256, 512)
+        quantise_x(0, 0, 256)
+        lay_x(1)
+        quantise_x(1, 0, 256)
+        quantise_x(1, 256, 256)
         gather_words(0, 0, 512)
         gather_words(0, 512, 512)
+        lay_x(2)
         lay_x(3)
+        quantise_x(2)
         lay_x(4)
         quantise_x(3)
-        lay_x(5)
         quantise_x(4)
-        quantise_x(5)
         gather_words(1, 0, 256)
         gather_bytes(0, 256)
         gather_words(1, 256, 768)
         weights(0)
         gather_bytes(256, 768, tag="w_bf0")
         weights(1)
-        expert(0)
+        multiply(0)
+        activate(0)
         scatter(0, 0)
         weights(2)
-        expert(1)
+        multiply(1)
+        activate(1)
         scatter(0, 1)
         scatter(1, 0)
         weights(3)
         scatter(1, 1)
-        expert(2)
-        expert(3)
+        multiply(2)
+        activate(2)
+        multiply(3)
+        activate(3)
         scatter(2, 0)
         scatter(2, 1)
         scatter(3, 0)
         scatter(3, 1)
-        finish(0, (640, 640))
-        finish(1, (512, 512, 256))
+        finish(0, 0, 640, 640)
+        finish(1, 0, 512, 512, 256)

from contextlib import ExitStack

import concourse.mybir as mybir

K, T, E, C, N = 1024, 1280, 4, 256, 256
P = 128
PACK = 4
PASSES = K // (P * PACK)
HALVES = N // P
FLOPS = 2 * K * N * E * C

F32 = mybir.dt.float32
BF16 = mybir.dt.bfloat16
U32 = mybir.dt.uint32
U16 = mybir.dt.uint16
U8 = mybir.dt.uint8
FP8X4 = mybir.dt.float8_e4m3fn_x4
ADD, MULT = mybir.AluOpType.add, mybir.AluOpType.mult
COPY = mybir.ActivationFunctionType.Copy
RELU = mybir.ActivationFunctionType.Relu
SQUARE = mybir.ActivationFunctionType.Square

X_CHUNKS = [
    (0, 0, [("s", 256), ("v", 512)]),
    (0, 768, [("v", 256), ("s", 256)]),
    (1, 0, [("s", 384), ("v", 128)]),
    (1, 512, [("s", 256), ("v", 256)]),
    (1, 1024, [("s", 128), ("v", 128)]),
]

AFTER = {(0, 0): "w_raw1_0", (0, 1): "w_raw1_1", (1, 0): "w_raw2_1", (2, 0): "w_raw3_1"}


def interleaved(view):
    return view.rearrange("p (c i) t -> p c t i", i=4)


def rows(view):
    return view.rearrange("p t (c i) -> p c t i", i=4)


def tile_moe_res_lin_relu2_kernel(tc, xT, xr, w, b, gate, offs, out):
    nc = tc.nc
    x_view = xT.rearrange("(a p j) t -> a p j t", p=P, j=PACK)
    w_view = w.rearrange("e (a p j) n -> e a p j n", p=P, j=PACK)
    xr_view = xr.rearrange("(h p) t -> h p t", p=P)
    gate_view = gate.rearrange("(h p) s -> h p s", p=P)
    out_view = out.rearrange("(h p) t -> h p t", p=P)

    with ExitStack() as ctx:
        keep = ctx.enter_context(tc.tile_pool(name="keep", bufs=1))
        psum = ctx.enter_context(tc.psum_pool(name="psum", bufs=1))

        offs_sb = keep.tile([P, E * C // 16], U16, name="offs_sb")
        x_codes = [keep.tile([P, T], U32, name=f"x_codes{a}", align_bytes=64) for a in range(PASSES)]
        x_scales = keep.tile([P, T], U8, name="x_scales", align_bytes=64)
        window = [keep.tile([P, T], F32, name=f"window{h}") for h in range(HALVES)]
        xr_sb = [keep.tile([P, T], F32, name=f"xr{h}") for h in range(HALVES)]
        b_sb = keep.tile([P, HALVES, E], F32, name="b_sb")

        nc.gpsimd.memset(x_scales[:], 0)
        for h in range(HALVES):
            nc.gpsimd.memset(window[h][:], 0.0)

        x_raw, w_raw, gate_sb = [], {}, {}

        def load_x(i):
            a, t0, pieces = X_CHUNKS[i]
            n = sum(m for eng, m in pieces)
            raw = keep.tile([P, PACK, n], F32, name=f"x_raw{i}")
            nc.sync.dma_start(out=raw[:], in_=x_view[a][:, :, t0 : t0 + n])
            x_raw.append(raw)

        def load_w(e, a):
            raw = keep.tile([P, PACK, N], F32, name=f"w_raw{e}_{a}", tag=f"w_raw{e}_{a}")
            nc.sync.dma_start(out=raw[:], in_=w_view[e, a])
            w_raw[e, a] = raw

        def load_gate(h, e0, e1):
            g = keep.tile([P, (e1 - e0) * C], F32, name=f"gate{h}_{e0}")
            nc.sync.dma_start(out=g[:], in_=gate_view[h][:, e0 * C : e1 * C])
            for e in range(e0, e1):
                gate_sb[e, h] = g[:, (e - e0) * C : (e - e0 + 1) * C]

        def load_xr(h):
            nc.sync.dma_start(out=xr_sb[h][:], in_=xr_view[h])

        def load_b():
            nc.sync.dma_start(out=b_sb[:], in_=b.rearrange("(h p) e -> p h e", p=P))

        load_x(0)
        load_x(1)
        nc.sync.dma_start(offs_sb[:], offs)
        load_x(2)
        load_x(3)
        load_x(4)
        load_w(0, 0)
        load_w(0, 1)
        load_b()
        load_w(1, 0)
        load_w(1, 1)
        load_gate(0, 0, 2)
        load_gate(1, 0, 2)
        load_w(2, 0)
        load_w(2, 1)
        load_w(3, 0)
        load_w(3, 1)
        load_gate(0, 2, 4)
        load_gate(1, 2, 4)
        load_xr(0)
        load_xr(1)

        x_words, x_bytes = {}, {}

        def gather_words(a, s0, n, tag=None):
            got = keep.tile([P, n], U32, name=f"words{a}_{s0}", tag=tag or f"words{a}_{s0}", align_bytes=64)
            nc.vector.tensor_copy(got[:], x_codes[a][:].indirect(offs_sb[:, s0 // 16 : (s0 + n) // 16]))
            for e in range(s0 // C, (s0 + n) // C):
                x_words[a, e] = got[:, e * C - s0 : (e + 1) * C - s0]

        def gather_bytes(s0, n, tag=None):
            got = keep.tile([P, n], U8, name=f"bytes_{s0}", tag=tag or f"bytes_{s0}", align_bytes=64)
            nc.vector.tensor_copy(got[:], x_scales[:].indirect(offs_sb[:, s0 // 16 : (s0 + n) // 16]))
            for e in range(s0 // C, (s0 + n) // C):
                for a in range(PASSES):
                    x_bytes[a, e] = got[4 * a :, e * C - s0 : (e + 1) * C - s0]

        x_bf = {}

        def lay_x(i):
            a, t0, pieces = X_CHUNKS[i]
            n = sum(m for eng, m in pieces)
            bf = keep.tile([P, n, PACK], BF16, name=f"x_bf{i}", align_bytes=64)
            u0 = 0
            for eng, m in pieces:
                dst = interleaved(bf[:, u0 : u0 + m, :])
                src = rows(x_raw[i][:, :, u0 : u0 + m])
                if eng == "s":
                    nc.scalar.activation(dst, src, COPY)
                else:
                    nc.vector.tensor_copy(dst, src)
                u0 += m
            x_bf[i] = bf

        def quantise_x(i, u0=0, n=None):
            a, t0, pieces = X_CHUNKS[i]
            n = n or sum(m for eng, m in pieces)
            cols = slice(t0 + u0, t0 + u0 + n)
            nc.vector.quantize_mx(
                out=x_codes[a][:, cols].bitcast(FP8X4),
                scales=x_scales[4 * a :, cols],
                in_=x_bf[i][:, u0 : u0 + n, :].rearrange("p n t -> p (n t)"),
            )

        w_codes, w_scales = {}, {}

        def weights(e):
            bf = keep.tile([P, PASSES, N, PACK], BF16, name=f"w_bf{e}", tag=f"w_bf{e}", align_bytes=64)
            for a in range(PASSES):
                if (e, a) in ():
                    nc.gpsimd.tensor_scalar(interleaved(bf[:, a]), rows(w_raw[e, a][:]), 1.0, 0.0, MULT, ADD)
                elif (e, a) in ():
                    nc.vector.tensor_copy(interleaved(bf[:, a]), rows(w_raw[e, a][:]))
                else:
                    for n0 in range(0, N, 256):
                        cols = slice(n0, n0 + 256)
                        nc.scalar.activation(interleaved(bf[:, a, cols, :]), rows(w_raw[e, a][:, :, cols]), COPY)
            codes = keep.tile([P, PASSES * N], U32, name=f"w_codes{e}", align_bytes=64)
            scales = keep.tile([P, PASSES * N], U8, name=f"w_scales{e}", align_bytes=64)
            nc.vector.quantize_mx(
                out=codes[:].bitcast(FP8X4), scales=scales[:], in_=bf[:].rearrange("p a n t -> p (a n t)")
            )
            w_codes[e], w_scales[e] = codes, scales

        squares, accs = {}, {}

        def multiply(e):
            for h in range(HALVES):
                acc = psum.tile([P, C], F32, name=f"acc{e}_{h}")
                accs[e, h] = acc
                for a in range(PASSES):
                    cols = slice(a * N + h * P, a * N + (h + 1) * P)
                    nc.tensor.matmul_mx(
                        out=acc[:],
                        lhsT=w_codes[e][:, cols].bitcast(FP8X4),
                        lhsT_scale=w_scales[e][:, cols],
                        rhs=x_words[a, e].bitcast(FP8X4),
                        rhs_scale=x_bytes[a, e],
                        start=(a == 0),
                        stop=(a == PASSES - 1),
                    )

        def activate(e, halves=(0, 1)):
            for h in halves:
                r = keep.tile([P, C], F32, name=f"relu{e}_{h}", tag=AFTER.get((e, h), f"relu{e}_{h}"))
                s = keep.tile([P, C], F32, name=f"square{e}_{h}")
                nc.scalar.activation(r[:], accs[e, h][:], RELU, bias=b_sb[:, h, e : e + 1])
                nc.scalar.activation(s[:], r[:], SQUARE)
                squares[e, h] = s

        def scatter(e, h):
            nc.vector.tensor_tensor(
                window[h][:].indirect(offs_sb[:, e * C // 16 : (e + 1) * C // 16]), squares[e, h][:], gate_sb[e, h], MULT
            )

        total = [keep.tile([P, T], F32, name=f"total{h}") for h in range(HALVES)]

        def finish(h, t0, *widths):
            for n in widths:
                cols = slice(t0, t0 + n)
                nc.vector.tensor_tensor(total[h][:, cols], window[h][:, cols], xr_sb[h][:, cols], ADD)
                nc.sync.dma_start(out=out_view[h][:, cols], in_=total[h][:, cols])
                t0 += n

        lay_x(0)
        quantise_x(0, 256, 512)
        quantise_x(0, 0, 256)
        lay_x(1)
        quantise_x(1, 0, 256)
        quantise_x(1, 256, 256)
        gather_words(0, 0, 512)
        gather_words(0, 512, 512)
        lay_x(2)
        lay_x(3)
        quantise_x(2)
        lay_x(4)
        quantise_x(3)
        quantise_x(4)
        gather_words(1, 0, 256)
        gather_bytes(0, 256)
        gather_words(1, 256, 768)
        weights(0)
        gather_bytes(256, 768, tag="w_bf0")
        weights(1)
        multiply(0)
        activate(0)
        scatter(0, 0)
        weights(2)
        multiply(1)
        activate(1)
        scatter(0, 1)
        scatter(1, 0)
        weights(3)
        scatter(1, 1)
        multiply(2)
        activate(2)
        multiply(3)
        activate(3)
        scatter(2, 0)
        scatter(2, 1)
        scatter(3, 0)
        scatter(3, 1)
        finish(0, 0, 640, 640)
        finish(1, 0, 512, 512, 256)
